import numpy as np
import ml_dtypes

BF16 = ml_dtypes.bfloat16


def bf(x):
    return np.asarray(x, np.float32).astype(BF16)


def f32(x):
    return np.asarray(x, np.float32)


def f64(x):
    return np.asarray(x).astype(np.float64)


def striped(idx):
    return np.tile(idx.reshape(-1, 16).T, (8, 1))


S, K, M, N = 256, 512, 512, 192


def setup_inputs():
    return {"base": bf(np.random.standard_normal((M, S))), "x": bf(np.random.standard_normal((K, N))), "w": bf(np.random.standard_normal((K, M)) / np.sqrt(K)), "b": f32(0.5 * np.random.standard_normal((M, 1))), "offs": striped(np.random.permutation(S)[:N])}


def reference(base, x, w, b, offs):
    idx = offs[:16].T.reshape(-1)
    z = f64(base).copy()
    z[:, idx] += f64(w).T @ f64(x)
    return np.maximum(z + f64(b), 0.0)

@@ -1,0 +1,57 @@
+import concourse.mybir as mybir
+from concourse.masks import make_identity
+
+BF16, F32, U16 = mybir.dt.bfloat16, mybir.dt.float32, mybir.dt.uint16
+ADD, MAX = mybir.AluOpType.add, mybir.AluOpType.max
+RELU = mybir.ActivationFunctionType.Relu
+
+P = 128
+S, K, M, N = 256, 512, 512, 192
+KB = K // P
+MB = M // P
+
+FLOPS = 2 * K * M * N
+
+
+def tile_scatter_matmul_kernel(tc, base, x, w, b, offs, out):
+    nc = tc.nc
+    with (
+        tc.tile_pool(name="held", bufs=1) as held,
+        tc.psum_pool(name="banks", bufs=1) as banks,
+    ):
+        offsets = held.tile([P, N // 16], U16, name="offsets")
+        nc.sync.dma_start(offsets[:], offs)
+
+        base_sb = held.tile([P, MB, S], BF16, name="base_sb")
+        nc.scalar.dma_start(base_sb[:], base.rearrange("(mb p) s -> p mb s", p=P))
+        x_sb = held.tile([P, KB, N], BF16, name="x_sb")
+        nc.sync.dma_start(x_sb[:], x.rearrange("(kb p) n -> p kb n", p=P))
+        w_sb = held.tile([P, KB, M], BF16, name="w_sb")
+        nc.sync.dma_start(w_sb[:], w.rearrange("(kb p) m -> p kb m", p=P))
+        bias_sb = held.tile([P, MB], F32, name="bias_sb")
+        with nc.allow_non_contiguous_dma(reason="one float32 to a partition and block: 512 values in all"):
+            nc.scalar.dma_start(bias_sb[:], b.rearrange("(mb p) o -> p (mb o)", p=P))
+
+        ident = held.tile([P, P], BF16, name="ident")
+        make_identity(nc, ident[:])
+
+        windows = [banks.tile([P, S], F32, name=f"window{mb}") for mb in range(MB)]
+        for mb in range(MB):
+            nc.tensor.matmul(windows[mb][:], ident[:], base_sb[:, mb, :], start=True, stop=False)
+
+        for mb in range(MB):
+            for kb in range(KB):
+                nc.tensor.matmul(
+                    windows[mb][:].indirect(offsets[:]),
+                    w_sb[:, kb, mb * P : (mb + 1) * P],
+                    x_sb[:, kb, :],
+                    start=False,
+                    stop=(kb == KB - 1),
+                )
+            out_sb = held.tile([P, S], F32, name=f"out_sb{mb}")
+            if mb % 2 == 0:
+                nc.scalar.activation(out_sb[:], windows[mb][:], RELU, bias=bias_sb[:, mb : mb + 1])
+                nc.scalar.dma_start(out[mb * P : (mb + 1) * P, :], out_sb[:])
+            else:
+                nc.vector.tensor_scalar(out_sb[:], windows[mb][:], bias_sb[:, mb : mb + 1], 0.0, ADD, MAX)
+                nc.sync.dma_start(out[mb * P : (mb + 1) * P, :], out_sb[:])

@@ -26,8 +26,10 @@ def tile_scatter_matmul_kernel(tc, base, x, w, b, offs, out):
         nc.scalar.dma_start(base_sb[:], base.rearrange("(mb p) s -> p mb s", p=P))
         x_sb = held.tile([P, KB, N], BF16, name="x_sb")
         nc.sync.dma_start(x_sb[:], x.rearrange("(kb p) n -> p kb n", p=P))
-        w_sb = held.tile([P, KB, M], BF16, name="w_sb")
-        nc.sync.dma_start(w_sb[:], w.rearrange("(kb p) m -> p kb m", p=P))
+        w_sb = [held.tile([P, M], BF16, name=f"w_sb{kb}") for kb in range(KB)]
+        for kb in range(KB):
+            queue = nc.sync if kb % 2 == 0 else nc.scalar
+            queue.dma_start(w_sb[kb][:], w[kb * P : (kb + 1) * P, :])
         bias_sb = held.tile([P, MB], F32, name="bias_sb")
         with nc.allow_non_contiguous_dma(reason="one float32 to a partition and block: 512 values in all"):
             nc.scalar.dma_start(bias_sb[:], b.rearrange("(mb p) o -> p (mb o)", p=P))
@@ -39,15 +41,20 @@ def tile_scatter_matmul_kernel(tc, base, x, w, b, offs, out):
         for mb in range(MB):
             nc.tensor.matmul(windows[mb][:], ident[:], base_sb[:, mb, :], start=True, stop=False)
 
+        def scattered_matmul(mb, kb):
+            nc.tensor.matmul(
+                windows[mb][:].indirect(offsets[:]),
+                w_sb[kb][:, mb * P : (mb + 1) * P],
+                x_sb[:, kb, :],
+                start=False,
+                stop=(kb == KB - 1),
+            )
+
         for mb in range(MB):
-            for kb in range(KB):
-                nc.tensor.matmul(
-                    windows[mb][:].indirect(offsets[:]),
-                    w_sb[:, kb, mb * P : (mb + 1) * P],
-                    x_sb[:, kb, :],
-                    start=False,
-                    stop=(kb == KB - 1),
-                )
+            scattered_matmul(mb, 0)
+        for mb in range(MB):
+            for kb in range(1, KB):
+                scattered_matmul(mb, kb)
             out_sb = held.tile([P, S], F32, name=f"out_sb{mb}")
             if mb % 2 == 0:
                 nc.scalar.activation(out_sb[:], windows[mb][:], RELU, bias=bias_sb[:, mb : mb + 1])

@@ -9,6 +9,8 @@ P = 128
 S, K, M, N = 256, 512, 512, 192
 KB = K // P
 MB = M // P
+BANK = 512
+WARM_UPS = 4
 
 FLOPS = 2 * K * M * N
 
@@ -19,6 +21,12 @@ def tile_scatter_matmul_kernel(tc, base, x, w, b, offs, out):
         tc.tile_pool(name="held", bufs=1) as held,
         tc.psum_pool(name="banks", bufs=1) as banks,
     ):
+        zeros = held.tile([P, BANK], BF16, name="zeros")
+        nc.gpsimd.memset(zeros[:], 0.0)
+        unread = banks.tile([P, BANK], F32, name="unread")
+        for i in range(WARM_UPS):
+            nc.tensor.matmul(unread[:], zeros[:, 0:P], zeros[:], start=True, stop=True)
+
         offsets = held.tile([P, N // 16], U16, name="offsets")
         nc.sync.dma_start(offsets[:], offs)
 

@@ -27,20 +27,18 @@ def tile_scatter_matmul_kernel(tc, base, x, w, b, offs, out):
         for i in range(WARM_UPS):
             nc.tensor.matmul(unread[:], zeros[:, 0:P], zeros[:], start=True, stop=True)
 
+        base_sb = held.tile([P, MB, S], BF16, name="base_sb")
+        nc.sync.dma_start(base_sb[:], base.rearrange("(mb p) s -> p mb s", p=P))
         offsets = held.tile([P, N // 16], U16, name="offsets")
         nc.sync.dma_start(offsets[:], offs)
-
-        base_sb = held.tile([P, MB, S], BF16, name="base_sb")
-        nc.scalar.dma_start(base_sb[:], base.rearrange("(mb p) s -> p mb s", p=P))
         x_sb = held.tile([P, KB, N], BF16, name="x_sb")
         nc.sync.dma_start(x_sb[:], x.rearrange("(kb p) n -> p kb n", p=P))
         w_sb = [held.tile([P, M], BF16, name=f"w_sb{kb}") for kb in range(KB)]
         for kb in range(KB):
-            queue = nc.sync if kb % 2 == 0 else nc.scalar
-            queue.dma_start(w_sb[kb][:], w[kb * P : (kb + 1) * P, :])
+            nc.sync.dma_start(w_sb[kb][:], w[kb * P : (kb + 1) * P, :])
         bias_sb = held.tile([P, MB], F32, name="bias_sb")
         with nc.allow_non_contiguous_dma(reason="one float32 to a partition and block: 512 values in all"):
-            nc.scalar.dma_start(bias_sb[:], b.rearrange("(mb p) o -> p (mb o)", p=P))
+            nc.sync.dma_start(bias_sb[:], b.rearrange("(mb p) o -> p (mb o)", p=P))
 
         ident = held.tile([P, P], BF16, name="ident")
         make_identity(nc, ident[:])

@@ -32,10 +32,11 @@ def tile_scatter_matmul_kernel(tc, base, x, w, b, offs, out):
         offsets = held.tile([P, N // 16], U16, name="offsets")
         nc.sync.dma_start(offsets[:], offs)
         x_sb = held.tile([P, KB, N], BF16, name="x_sb")
-        nc.sync.dma_start(x_sb[:], x.rearrange("(kb p) n -> p kb n", p=P))
+        nc.sync.dma_start(x_sb[:], x.rearrange("(p kb) n -> p kb n", kb=KB))
+        w_blocks = w.rearrange("(p kb) m -> p kb m", kb=KB)
         w_sb = [held.tile([P, M], BF16, name=f"w_sb{kb}") for kb in range(KB)]
         for kb in range(KB):
-            nc.sync.dma_start(w_sb[kb][:], w[kb * P : (kb + 1) * P, :])
+            nc.sync.dma_start(w_sb[kb][:], w_blocks[:, kb, :])
         bias_sb = held.tile([P, MB], F32, name="bias_sb")
         with nc.allow_non_contiguous_dma(reason="one float32 to a partition and block: 512 values in all"):
             nc.sync.dma_start(bias_sb[:], b.rearrange("(mb p) o -> p (mb o)", p=P))

@@ -21,11 +21,13 @@ def tile_scatter_matmul_kernel(tc, base, x, w, b, offs, out):
         tc.tile_pool(name="held", bufs=1) as held,
         tc.psum_pool(name="banks", bufs=1) as banks,
     ):
-        zeros = held.tile([P, BANK], BF16, name="zeros")
+        zeros = held.tile([P, P], BF16, name="zeros")
         nc.gpsimd.memset(zeros[:], 0.0)
-        unread = banks.tile([P, BANK], F32, name="unread")
+        unread = banks.tile([P, BANK // P, P], F32, name="unread")
         for i in range(WARM_UPS):
-            nc.tensor.matmul(unread[:], zeros[:, 0:P], zeros[:], start=True, stop=True)
+            nc.tensor.matmul(
+                unread[:], zeros[:], zeros[:].unsqueeze(1).to_broadcast([P, BANK // P, P]), start=True, stop=True
+            )
 
         base_sb = held.tile([P, MB, S], BF16, name="base_sb")
         nc.sync.dma_start(base_sb[:], base.rearrange("(mb p) s -> p mb s", p=P))

@@ -10,7 +10,7 @@ S, K, M, N = 256, 512, 512, 192
 KB = K // P
 MB = M // P
 BANK = 512
-WARM_UPS = 4
+WARM_UPS = 3
 
 FLOPS = 2 * K * M * N
 

@@ -9,6 +9,7 @@ P = 128
 S, K, M, N = 256, 512, 512, 192
 KB = K // P
 MB = M // P
+HALF = 2
 BANK = 512
 WARM_UPS = 3
 
@@ -29,15 +30,19 @@ def tile_scatter_matmul_kernel(tc, base, x, w, b, offs, out):
                 unread[:], zeros[:], zeros[:].unsqueeze(1).to_broadcast([P, BANK // P, P]), start=True, stop=True
             )
 
-        base_sb = held.tile([P, MB, S], BF16, name="base_sb")
-        nc.sync.dma_start(base_sb[:], base.rearrange("(mb p) s -> p mb s", p=P))
+        base_blocks = base.rearrange("(mb p) s -> p mb s", p=P)
+        base_sb = [held.tile([P, HALF, S], BF16, name=f"base_sb{h}") for h in range(2)]
+        for h in range(2):
+            nc.sync.dma_start(base_sb[h][:], base_blocks[:, h * HALF : (h + 1) * HALF, :])
         offsets = held.tile([P, N // 16], U16, name="offsets")
         nc.sync.dma_start(offsets[:], offs)
-        x_sb = held.tile([P, KB, N], BF16, name="x_sb")
-        nc.sync.dma_start(x_sb[:], x.rearrange("(p kb) n -> p kb n", kb=KB))
+        x_blocks = x.rearrange("(p kb) n -> p kb n", kb=KB)
         w_blocks = w.rearrange("(p kb) m -> p kb m", kb=KB)
+        x_sb = [held.tile([P, HALF, N], BF16, name=f"x_sb{h}") for h in range(2)]
         w_sb = [held.tile([P, M], BF16, name=f"w_sb{kb}") for kb in range(KB)]
         for kb in range(KB):
+            if kb % HALF == 0:
+                nc.sync.dma_start(x_sb[kb // HALF][:], x_blocks[:, kb : kb + HALF, :])
             nc.sync.dma_start(w_sb[kb][:], w_blocks[:, kb, :])
         bias_sb = held.tile([P, MB], F32, name="bias_sb")
         with nc.allow_non_contiguous_dma(reason="one float32 to a partition and block: 512 values in all"):
@@ -48,13 +53,13 @@ def tile_scatter_matmul_kernel(tc, base, x, w, b, offs, out):
 
         windows = [banks.tile([P, S], F32, name=f"window{mb}") for mb in range(MB)]
         for mb in range(MB):
-            nc.tensor.matmul(windows[mb][:], ident[:], base_sb[:, mb, :], start=True, stop=False)
+            nc.tensor.matmul(windows[mb][:], ident[:], base_sb[mb // HALF][:, mb % HALF, :], start=True, stop=False)
 
         def scattered_matmul(mb, kb):
             nc.tensor.matmul(
                 windows[mb][:].indirect(offsets[:]),
                 w_sb[kb][:, mb * P : (mb + 1) * P],
-                x_sb[:, kb, :],
+                x_sb[kb // HALF][:, kb % HALF, :],
                 start=False,
                 stop=(kb == KB - 1),
             )

@@ -70,7 +70,7 @@ def tile_scatter_matmul_kernel(tc, base, x, w, b, offs, out):
             for kb in range(1, KB):
                 scattered_matmul(mb, kb)
             out_sb = held.tile([P, S], F32, name=f"out_sb{mb}")
-            if mb % 2 == 0:
+            if mb % 2 == 1:
                 nc.scalar.activation(out_sb[:], windows[mb][:], RELU, bias=bias_sb[:, mb : mb + 1])
                 nc.scalar.dma_start(out[mb * P : (mb + 1) * P, :], out_sb[:])
             else:

@@ -30,6 +30,9 @@ def tile_scatter_matmul_kernel(tc, base, x, w, b, offs, out):
                 unread[:], zeros[:], zeros[:].unsqueeze(1).to_broadcast([P, BANK // P, P]), start=True, stop=True
             )
 
+        early_relu = held.tile([P, 1], F32, name="early_relu")
+        nc.scalar.activation(early_relu[:], zeros[:, 0:1], RELU)
+
         base_blocks = base.rearrange("(mb p) s -> p mb s", p=P)
         base_sb = [held.tile([P, HALF, S], BF16, name=f"base_sb{h}") for h in range(2)]
         for h in range(2):

@@ -9,7 +9,7 @@ P = 128
 S, K, M, N = 256, 512, 512, 192
 KB = K // P
 MB = M // P
-HALF = 2
+HALF = MB // 2
 BANK = 512
 WARM_UPS = 3
 
@@ -41,11 +41,13 @@ def tile_scatter_matmul_kernel(tc, base, x, w, b, offs, out):
         nc.sync.dma_start(offsets[:], offs)
         x_blocks = x.rearrange("(p kb) n -> p kb n", kb=KB)
         w_blocks = w.rearrange("(p kb) m -> p kb m", kb=KB)
-        x_sb = [held.tile([P, HALF, N], BF16, name=f"x_sb{h}") for h in range(2)]
+        x_first = held.tile([P, N], BF16, name="x_first")
+        x_rest = held.tile([P, KB - 1, N], BF16, name="x_rest")
         w_sb = [held.tile([P, M], BF16, name=f"w_sb{kb}") for kb in range(KB)]
-        for kb in range(KB):
-            if kb % HALF == 0:
-                nc.sync.dma_start(x_sb[kb // HALF][:], x_blocks[:, kb : kb + HALF, :])
+        nc.sync.dma_start(x_first[:], x_blocks[:, 0, :])
+        nc.sync.dma_start(w_sb[0][:], w_blocks[:, 0, :])
+        nc.sync.dma_start(x_rest[:], x_blocks[:, 1:KB, :])
+        for kb in range(1, KB):
             nc.sync.dma_start(w_sb[kb][:], w_blocks[:, kb, :])
         bias_sb = held.tile([P, MB], F32, name="bias_sb")
         with nc.allow_non_contiguous_dma(reason="one float32 to a partition and block: 512 values in all"):
@@ -62,16 +64,12 @@ def tile_scatter_matmul_kernel(tc, base, x, w, b, offs, out):
             nc.tensor.matmul(
                 windows[mb][:].indirect(offsets[:]),
                 w_sb[kb][:, mb * P : (mb + 1) * P],
-                x_sb[kb // HALF][:, kb % HALF, :],
+                x_first[:] if kb == 0 else x_rest[:, kb - 1, :],
                 start=False,
                 stop=(kb == KB - 1),
             )
 
-        for mb in range(MB):
-            scattered_matmul(mb, 0)
-        for mb in range(MB):
-            for kb in range(1, KB):
-                scattered_matmul(mb, kb)
+        def epilogue(mb):
             out_sb = held.tile([P, S], F32, name=f"out_sb{mb}")
             if mb % 2 == 1:
                 nc.scalar.activation(out_sb[:], windows[mb][:], RELU, bias=bias_sb[:, mb : mb + 1])
@@ -79,3 +77,17 @@ def tile_scatter_matmul_kernel(tc, base, x, w, b, offs, out):
             else:
                 nc.vector.tensor_scalar(out_sb[:], windows[mb][:], bias_sb[:, mb : mb + 1], 0.0, ADD, MAX)
                 nc.sync.dma_start(out[mb * P : (mb + 1) * P, :], out_sb[:])
+
+        for mb in reversed(range(MB)):
+            scattered_matmul(mb, 0)
+        scattered_matmul(0, 1)
+        for kb in range(1, KB):
+            scattered_matmul(1, kb)
+        epilogue(1)
+        for kb in range(2, KB):
+            scattered_matmul(0, kb)
+        epilogue(0)
+        for mb in range(2, MB):
+            for kb in range(1, KB):
+                scattered_matmul(mb, kb)
+            epilogue(mb)

@@ -9,7 +9,6 @@ P = 128
 S, K, M, N = 256, 512, 512, 192
 KB = K // P
 MB = M // P
-HALF = MB // 2
 BANK = 512
 WARM_UPS = 3
 
@@ -33,10 +32,9 @@ def tile_scatter_matmul_kernel(tc, base, x, w, b, offs, out):
         early_relu = held.tile([P, 1], F32, name="early_relu")
         nc.scalar.activation(early_relu[:], zeros[:, 0:1], RELU)
 
-        base_blocks = base.rearrange("(mb p) s -> p mb s", p=P)
-        base_sb = [held.tile([P, HALF, S], BF16, name=f"base_sb{h}") for h in range(2)]
-        for h in range(2):
-            nc.sync.dma_start(base_sb[h][:], base_blocks[:, h * HALF : (h + 1) * HALF, :])
+        base_sb = [held.tile([P, S], BF16, name=f"base_sb{mb}") for mb in range(MB)]
+        for mb in range(MB):
+            nc.sync.dma_start(base_sb[mb][:], base[mb * P : (mb + 1) * P, :])
         offsets = held.tile([P, N // 16], U16, name="offsets")
         nc.sync.dma_start(offsets[:], offs)
         x_blocks = x.rearrange("(p kb) n -> p kb n", kb=KB)
@@ -58,7 +56,7 @@ def tile_scatter_matmul_kernel(tc, base, x, w, b, offs, out):
 
         windows = [banks.tile([P, S], F32, name=f"window{mb}") for mb in range(MB)]
         for mb in range(MB):
-            nc.tensor.matmul(windows[mb][:], ident[:], base_sb[mb // HALF][:, mb % HALF, :], start=True, stop=False)
+            nc.tensor.matmul(windows[mb][:], ident[:], base_sb[mb][:], start=True, stop=False)
 
         def scattered_matmul(mb, kb):
             nc.tensor.matmul(

import concourse.mybir as mybir
from concourse.masks import make_identity

BF16, F32, U16 = mybir.dt.bfloat16, mybir.dt.float32, mybir.dt.uint16
ADD, MAX = mybir.AluOpType.add, mybir.AluOpType.max
RELU = mybir.ActivationFunctionType.Relu

P = 128
S, K, M, N = 256, 512, 512, 192
KB = K // P
MB = M // P
BANK = 512
WARM_UPS = 3

FLOPS = 2 * K * M * N


def tile_scatter_matmul_kernel(tc, base, x, w, b, offs, out):
    nc = tc.nc
    with (
        tc.tile_pool(name="held", bufs=1) as held,
        tc.psum_pool(name="banks", bufs=1) as banks,
    ):
        zeros = held.tile([P, P], BF16, name="zeros")
        nc.gpsimd.memset(zeros[:], 0.0)
        unread = banks.tile([P, BANK // P, P], F32, name="unread")
        for i in range(WARM_UPS):
            nc.tensor.matmul(
                unread[:], zeros[:], zeros[:].unsqueeze(1).to_broadcast([P, BANK // P, P]), start=True, stop=True
            )

        early_relu = held.tile([P, 1], F32, name="early_relu")
        nc.scalar.activation(early_relu[:], zeros[:, 0:1], RELU)

        base_sb = [held.tile([P, S], BF16, name=f"base_sb{mb}") for mb in range(MB)]
        for mb in range(MB):
            nc.sync.dma_start(base_sb[mb][:], base[mb * P : (mb + 1) * P, :])
        offsets = held.tile([P, N // 16], U16, name="offsets")
        nc.sync.dma_start(offsets[:], offs)
        x_blocks = x.rearrange("(p kb) n -> p kb n", kb=KB)
        w_blocks = w.rearrange("(p kb) m -> p kb m", kb=KB)
        x_first = held.tile([P, N], BF16, name="x_first")
        x_rest = held.tile([P, KB - 1, N], BF16, name="x_rest")
        w_sb = [held.tile([P, M], BF16, name=f"w_sb{kb}") for kb in range(KB)]
        nc.sync.dma_start(x_first[:], x_blocks[:, 0, :])
        nc.sync.dma_start(w_sb[0][:], w_blocks[:, 0, :])
        nc.sync.dma_start(x_rest[:], x_blocks[:, 1:KB, :])
        for kb in range(1, KB):
            nc.sync.dma_start(w_sb[kb][:], w_blocks[:, kb, :])
        bias_sb = held.tile([P, MB], F32, name="bias_sb")
        with nc.allow_non_contiguous_dma(reason="one float32 to a partition and block: 512 values in all"):
            nc.sync.dma_start(bias_sb[:], b.rearrange("(mb p) o -> p (mb o)", p=P))

        ident = held.tile([P, P], BF16, name="ident")
        make_identity(nc, ident[:])

        windows = [banks.tile([P, S], F32, name=f"window{mb}") for mb in range(MB)]
        for mb in range(MB):
            nc.tensor.matmul(windows[mb][:], ident[:], base_sb[mb][:], start=True, stop=False)

        def scattered_matmul(mb, kb):
            nc.tensor.matmul(
                windows[mb][:].indirect(offsets[:]),
                w_sb[kb][:, mb * P : (mb + 1) * P],
                x_first[:] if kb == 0 else x_rest[:, kb - 1, :],
                start=False,
                stop=(kb == KB - 1),
            )

        def epilogue(mb):
            out_sb = held.tile([P, S], F32, name=f"out_sb{mb}")
            if mb % 2 == 1:
                nc.scalar.activation(out_sb[:], windows[mb][:], RELU, bias=bias_sb[:, mb : mb + 1])
                nc.scalar.dma_start(out[mb * P : (mb + 1) * P, :], out_sb[:])
            else:
                nc.vector.tensor_scalar(out_sb[:], windows[mb][:], bias_sb[:, mb : mb + 1], 0.0, ADD, MAX)
                nc.sync.dma_start(out[mb * P : (mb + 1) * P, :], out_sb[:])

        for mb in reversed(range(MB)):
            scattered_matmul(mb, 0)
        scattered_matmul(0, 1)
        for kb in range(1, KB):
            scattered_matmul(1, kb)
        epilogue(1)
        for kb in range(2, KB):
            scattered_matmul(0, kb)
        epilogue(0)
        for mb in range(2, MB):
            for kb in range(1, KB):
                scattered_matmul(mb, kb)
            epilogue(mb)
